import numpy as np
import ml_dtypes


def mxq(x, axis, fmt="e4m3"):
    dtype, down = {"e4m3": (ml_dtypes.float8_e4m3fn, 7), "e5m2": (ml_dtypes.float8_e5m2, 14)}[fmt]
    v = np.moveaxis(np.asarray(x, np.float32).astype(ml_dtypes.bfloat16).astype(np.float64), axis, -1)
    blocks = v.reshape(v.shape[:-1] + (-1, 32))
    amax = np.abs(blocks).max(-1, keepdims=True)
    byte = np.maximum(np.where(amax > 0, np.frexp(amax)[1] - 1 + 127, 0) - down, 1)
    scale = np.exp2(byte - 127.0)
    codes = (blocks / scale).astype(np.float32).astype(dtype).astype(np.float64)
    return np.moveaxis((codes * scale).reshape(v.shape), -1, axis)


WIDE = False


def mx_kscale(k):
    if not WIDE:
        return np.ones(k)
    levels = np.array([10, -10, 5, -5, 0])
    if k % 512:
        return np.exp2(np.random.permutation(np.resize(levels, k // 32))).repeat(32)
    a = np.empty((k // 512, 16))
    for p in range(k // 512):
        a[p, :8] = np.random.permutation(np.resize(levels, 8))
        for g in range(8):
            far = levels[np.abs(levels - a[p, g]) >= 10]
            a[p, g + 8] = far[np.random.randint(len(far))]
    return np.exp2(a.ravel()).repeat(32)


def f64(x):
    return np.asarray(x).astype(np.float64)


def striped(idx):
    return np.tile(np.asarray(idx).reshape(-1, 16).T, (8, 1)).astype(np.uint16)


def unstriped(offs):
    return offs[:16].T.reshape(-1).astype(np.int64)


def striped8(idx):
    return np.asarray(idx).reshape(8, -1, 16).transpose(0, 2, 1).reshape(128, -1).astype(np.uint16)


def unstriped8(offs):
    return offs.reshape(8, 16, -1).transpose(0, 2, 1).reshape(8, -1).astype(np.int64)


def pick8(x, idx, run):
    r = np.arange(len(x))
    return x[r[:, None], idx[r % (8 * run) // run]]


E2M1 = np.array([0.0, 0.5, 1.0, 1.5, 2.0, 3.0, 4.0, 6.0, -0.0, -0.5, -1.0, -1.5, -2.0, -3.0, -4.0, -6.0])


def pack_weight(w, fmt):
    k, n = w.shape
    w = f64(np.asarray(w, np.float32).astype(ml_dtypes.bfloat16)).reshape(k // 32, 32, n)
    amax = np.abs(w).max(1)
    if fmt == "e4m3":
        byte = np.frexp(amax)[1] - 1 + 127 - 7
    else:
        mant, ex = np.frexp(amax / 6.0)
        byte = np.where(mant > 0.5, ex, ex - 1) + 127
    byte = np.clip(np.where(amax > 0, byte, 1), 1, 254)
    scaled = (w * np.exp2(127.0 - byte)[:, None, :]).reshape(k, n).astype(np.float32)
    by_word = np.ascontiguousarray(scaled.reshape(k // 512, 128, 4, n).transpose(0, 1, 3, 2))
    if fmt == "e4m3":
        words = by_word.astype(ml_dtypes.float8_e4m3fn).view(np.uint8)
    else:
        c = by_word.astype(ml_dtypes.float4_e2m1fn).view(np.uint8) & 0xF
        words = (c[..., 0::2] | (c[..., 1::2] << 4)).reshape(k // 512, 128, 2 * n)
    return np.ascontiguousarray(words), np.ascontiguousarray(byte.astype(np.uint8).reshape(k // 512, 16, n))


def unpack_weight(words, scales, fmt):
    g, _, n = scales.shape
    words = np.ascontiguousarray(words).reshape(g, 128, n, -1)
    if fmt == "e4m3":
        vals = words.view(ml_dtypes.float8_e4m3fn).astype(np.float64)
    else:
        nib = np.empty((g, 128, n, 4), np.uint8)
        nib[..., 0::2] = words & 0xF
        nib[..., 1::2] = words >> 4
        vals = E2M1[nib]
    vals = vals * np.repeat(np.exp2(scales.astype(np.float64) - 127.0), 8, axis=1)[..., None]
    return vals.transpose(0, 1, 3, 2).reshape(g * 512, n)


K, J, R, T, C, D, O, S, N, Z = 512, 512, 512, 2048, 1024, 1024, 512, 256, 256, 1024


def setup_inputs():
    n = np.random.standard_normal
    idx = np.random.permutation(T)[:J]
    idx2 = np.stack([np.random.permutation(C)[:J] for _ in range(8)])
    idx3 = np.stack([np.random.permutation(C)[:S] for _ in range(8)])
    idx4 = np.stack([np.random.permutation(D)[:S] for _ in range(8)])
    idx5 = np.stack([np.random.permutation(D)[:J] for _ in range(8)])
    idx6 = np.stack([np.random.permutation(D)[:O] for _ in range(8)])
    idx7 = np.random.permutation(Z)[:N]
    fk = mx_kscale(K)
    fr = mx_kscale(R)
    xtp = pack_weight(n((K, T)) * fk[:, None], "e2m1")
    wp = pack_weight(n((K, R)) * 1 / np.sqrt(K) / fk[:, None] * fr, "e4m3")
    w2p = pack_weight(n((K, R)) * 1 / np.sqrt(K) / fk[:, None] * fr, "e4m3")
    vsp = pack_weight(n((R, Z)) * 1 / np.sqrt(R) / fr[:, None], "e4m3")
    return {
        "xt_words": xtp[0],
        "xt_scales": xtp[1],
        "w_words": wp[0],
        "w_scales": wp[1],
        "w2_words": w2p[0],
        "w2_scales": w2p[1],
        "sa": (np.random.uniform(0.5, 1.6, (R, 1))).astype(np.float32),
        "sb": (np.random.uniform(0.5, 1.6, (R, 1))).astype(np.float32),
        "vs_words": vsp[0],
        "vs_scales": vsp[1],
        "offs": striped(idx),
        "offs2": striped8(idx2),
        "offs3": striped8(idx3),
        "offs4": striped8(idx4),
        "offs5": striped8(idx5),
        "offs6": striped8(idx6),
        "offs7": striped(idx7),
    }


def reference(xt_words, xt_scales, w_words, w_scales, w2_words, w2_scales, sa, sb, vs_words, vs_scales, offs, offs2, offs3, offs4, offs5, offs6, offs7):
    idx = unstriped(offs)
    idx2 = unstriped8(offs2)
    idx3 = unstriped8(offs3)
    idx4 = unstriped8(offs4)
    idx5 = unstriped8(offs5)
    idx6 = unstriped8(offs6)
    idx7 = unstriped(offs7)
    xtu = unpack_weight(xt_words, xt_scales, "e2m1")
    wu = unpack_weight(w_words, w_scales, "e4m3")
    w2u = unpack_weight(w2_words, w2_scales, "e4m3")
    vsu = unpack_weight(vs_words, vs_scales, "e4m3")
    xtidxg = xtu[:, idx]
    a = wu.T @ xtidxg
    b = w2u.T @ xtidxg
    pw = np.zeros((R, C))
    pw[np.arange(R)[:, None], idx2[np.arange(R) % 512 // 64]] = a
    h1 = pick8(pw, idx3, 64) * f64(sa)
    pv = np.zeros((R, D))
    pv[np.arange(R)[:, None], idx4[np.arange(R) % 512 // 64]] = h1
    pu = np.zeros((R, D))
    pu[np.arange(R)[:, None], idx5[np.arange(R) % 512 // 64]] = b
    pg = pv + pu
    hid = pick8(pg, idx6, 64) * f64(sb)
    vsidx7g = vsu[:, idx7]
    hidq = mxq(hid, 0, "e4m3")
    y = vsidx7g.T @ hidq
    return y

@@ -1,0 +1,217 @@
+from contextlib import ExitStack
+
+import concourse.mybir as mybir
+
+K, J, R, T, C, D, O, S, N, Z = 512, 512, 512, 2048, 1024, 1024, 512, 256, 256, 1024
+FLOPS = 2 * (2 * K * R * J + R * N * O)
+
+F32 = mybir.dt.float32
+BF16 = mybir.dt.bfloat16
+I32 = mybir.dt.int32
+U32 = mybir.dt.uint32
+U16 = mybir.dt.uint16
+U8 = mybir.dt.uint8
+FP8X4 = mybir.dt.float8_e4m3fn_x4
+FP4X4 = mybir.dt.float4_e2m1fn_x4
+COPY = mybir.ActivationFunctionType.Copy
+ADD = mybir.AluOpType.add
+
+P = 128
+PACK = 4
+QUADS = 4
+STRIPE = 16
+HALF = 256
+
+
+def tile_picked_tokens_plain_twin_relaysum_store_plain_kernel(
+    tc, xt_words, xt_scales, w_words, w_scales, w2_words, w2_scales, sa, sb, vs_words, vs_scales,
+    offs, offs2, offs3, offs4, offs5, offs6, offs7, out,
+):
+    nc = tc.nc
+    with ExitStack() as ctx:
+        keep = ctx.enter_context(tc.tile_pool(name="keep", bufs=1))
+        psum = ctx.enter_context(tc.psum_pool(name="psum", bufs=4))
+
+        def load_list(src, name):
+            lst = keep.tile(list(src.shape), U16, name=name)
+            nc.sync.dma_start(lst[:], src)
+            return lst
+
+        def entries(lst, first, count):
+            return lst[:, first // STRIPE : (first + count) // STRIPE]
+
+        def zero_plane(width, name, tag):
+            plane = keep.tile([P, width], U8, name=name, tag=tag, align_bytes=64)
+            nc.vector.memset(plane[:].bitcast(I32), 0)
+            return plane
+
+        def load_plane(plane, scales):
+            for q in range(QUADS):
+                nc.sync.dma_start(out=plane[32 * q : 32 * q + 4, :].bitcast(I32), in_=scales[0, 4 * q : 4 * q + 4, :].bitcast(I32))
+
+        def stage_scales(scales, name):
+            width = scales.shape[2]
+            staged = keep.tile([4, QUADS, width // 4], I32, name=name, tag="staged")
+            nc.sync.dma_start(out=staged[:], in_=scales[0].bitcast(I32).rearrange("(q r) c -> r q c", r=4))
+            return staged
+
+        def spread_plane(plane, staged):
+            for q in range(QUADS):
+                nc.vector.tensor_copy(out=plane[32 * q : 32 * q + 4, :].bitcast(I32), in_=staged[:, q, :])
+
+        def load_words(words, name):
+            width = words.shape[2]
+            raw = keep.tile([P, width], U32, name=name, tag="words", align_bytes=64)
+            nc.sync.dma_start(out=raw[:].bitcast(I32), in_=words[0].rearrange("p n t -> p (n t)").bitcast(I32))
+            return raw
+
+        def load_rows(vec, name):
+            col = keep.tile([P, PACK], F32, name=name)
+            nc.sync.dma_start(out=col[:], in_=vec.rearrange("(p t) one -> p (t one)", t=PACK))
+            return col
+
+        def deal(copy, raw, dealt, tiles):
+            copy(out=dealt[:, tiles, :], in_=raw[:].rearrange("p (m t) -> p t m", t=PACK)[:, tiles, :])
+
+        def zero_board(width, name, tag):
+            board = keep.tile([P, width], F32, name=name, tag=tag, align_bytes=64)
+            nc.vector.memset(board[:], 0.0)
+            return board
+
+        xs_win = zero_plane(T, "xs_win", "x_scales")
+        load_plane(xs_win, xt_scales)
+        l_tok = load_list(offs, "l_tok")
+        ws_staged = stage_scales(w_scales, "ws_staged")
+        l_put_a = load_list(offs2, "l_put_a")
+        l_get_relay = load_list(offs3, "l_get_relay")
+        xw_win = keep.tile([P, T], U16, name="xw_win", tag="x_words", align_bytes=64)
+        nc.sync.dma_start(out=xw_win[:].bitcast(I32), in_=xt_words[0].bitcast(I32))
+        ww_raw = load_words(w_words, "ww_raw")
+        sa_col = load_rows(sa, "sa_col")
+        l_put_b = load_list(offs5, "l_put_b")
+        l_put_relay = load_list(offs4, "l_put_relay")
+        l_get_hid = load_list(offs6, "l_get_hid")
+        sb_col = load_rows(sb, "sb_col")
+        l_store = load_list(offs7, "l_store")
+
+        ws_raw = zero_plane(R, "ws_raw", "plane")
+        pw = zero_board(C, "pw", "pw")
+        spread_plane(ws_raw, ws_staged)
+        ws = keep.tile([P, PACK, P], U8, name="ws", align_bytes=64)
+        ww = keep.tile([P, PACK, P], U32, name="ww", align_bytes=64)
+        deal(nc.vector.tensor_copy, ws_raw, ws, slice(0, 1))
+        deal(nc.scalar.copy, ww_raw, ww, slice(0, PACK))
+
+        xw = keep.tile([P, J], U16, name="xw", align_bytes=64)
+        xs = keep.tile([P, J], U8, name="xs", align_bytes=64)
+
+        def product(words, scales, t, first, count, dst, copy):
+            acc = psum.tile([P, count], F32, name="acc")
+            cols = slice(first, first + count)
+            nc.tensor.matmul_mx(
+                out=acc[:], lhsT=words[:, t, :].bitcast(FP8X4), lhsT_scale=scales[:, t, :],
+                rhs=xw[:, cols].bitcast(FP4X4), rhs_scale=xs[:, cols], start=True, stop=True,
+            )
+            copy(out=dst[:, cols], in_=acc[:])
+
+        a = [keep.tile([P, J], F32, name="a%d" % t) for t in range(PACK)]
+        b = [keep.tile([P, J], F32, name="b%d" % t) for t in range(PACK - 1)]
+        b.append(keep.tile([P, J], F32, name="b_last", tag="late", align_bytes=64))
+
+        for first in (0, HALF):
+            cols = slice(first, first + HALF)
+            nc.vector.tensor_copy(out=xw[:, cols], in_=xw_win[:].indirect(entries(l_tok, first, HALF)))
+            nc.vector.tensor_copy(out=xs[:, cols], in_=xs_win[:].indirect(entries(l_tok, first, HALF)))
+            product(ww, ws, 0, first, HALF, a[0], nc.scalar.copy if first == 0 else nc.vector.tensor_copy)
+        deal(nc.vector.tensor_copy, ws_raw, ws, slice(1, PACK))
+
+        w2w_raw = load_words(w2_words, "w2w_raw")
+        w2s_staged = stage_scales(w2_scales, "w2s_staged")
+        w2s_raw = zero_plane(R, "w2s_raw", "plane")
+        spread_plane(w2s_raw, w2s_staged)
+        w2s = keep.tile([P, PACK, P], U8, name="w2s", align_bytes=64)
+        w2w = keep.tile([P, PACK, P], U32, name="w2w", align_bytes=64)
+        deal(nc.vector.tensor_copy, w2s_raw, w2s, slice(0, PACK))
+        deal(nc.vector.tensor_copy, w2w_raw, w2w, slice(0, PACK))
+        pu = zero_board(D, "pu", "x_words")
+        pv = zero_board(D, "pv", "x_scales")
+        product(w2w, w2s, 0, 0, J, b[0], nc.vector.tensor_copy)
+        for t in range(1, PACK):
+            product(ww, ws, t, 0, J, a[t], nc.vector.tensor_copy)
+            product(w2w, w2s, t, 0, J, b[t], nc.vector.tensor_copy)
+
+        vsw_win = load_words(vs_words, "vsw_win")
+        vss_staged = stage_scales(vs_scales, "vss_staged")
+        vss_win = zero_plane(Z, "vss_win", "plane")
+        spread_plane(vss_win, vss_staged)
+        vw = keep.tile([P, N], U32, name="vw", align_bytes=64)
+        vsc = keep.tile([P, N], U8, name="vsc", align_bytes=64)
+        nc.vector.tensor_copy(out=vw[:], in_=vsw_win[:].indirect(l_store[:]))
+        nc.vector.tensor_copy(out=vsc[:], in_=vss_win[:].indirect(l_store[:]))
+
+        h1 = keep.tile([P, S], F32, name="h1")
+        pg = [keep.tile([P, D], F32, name="pg%d" % t) for t in range(PACK)]
+        hid = {}
+
+        def read_board(t, h, tag):
+            if t % 2 == 0:
+                hid[(h, t // 2)] = keep.tile([P, 2, HALF], BF16, name="hid%d%d" % (h, t // 2), tag=tag, align_bytes=64)
+            nc.scalar.activation(
+                out=hid[(h, t // 2)][:, t % 2, :], in_=pg[t][:].indirect(entries(l_get_hid, h * HALF, HALF)),
+                func=COPY, scale=sb_col[:, t : t + 1],
+            )
+
+        grouped = [keep.tile([P, HALF, PACK], BF16, name="grouped%d" % h, align_bytes=64) for h in range(2)]
+
+        def weave(h, pair, cols):
+            nc.vector.tensor_copy(
+                out=grouped[h][:, cols, 2 * pair : 2 * pair + 2], in_=hid[(h, pair)][:, :, cols].rearrange("p t o -> p o t")
+            )
+
+        for t in range(PACK):
+            for first, count in ((0, HALF), (HALF, HALF)) if t == 0 else ((0, J),):
+                nc.scalar.activation(
+                    out=pw[:].indirect(entries(l_put_a, first, count)), in_=a[t][:, first : first + count], func=COPY
+                )
+            if t > 0:
+                read_board(t - 1, 0, "hid_first%d" % ((t - 1) // 2))
+            nc.scalar.activation(out=h1[:], in_=pw[:].indirect(l_get_relay[:]), func=COPY, scale=sa_col[:, t : t + 1])
+            nc.scalar.activation(out=pu[:].indirect(l_put_b[:]), in_=b[t][:], func=COPY)
+            nc.scalar.activation(out=pv[:].indirect(l_put_relay[:]), in_=h1[:], func=COPY)
+            nc.vector.tensor_tensor(out=pg[t][:], in0=pv[:], in1=pu[:], op=ADD)
+
+        def finish(h):
+            codes = keep.tile([P, HALF], U32, name="codes%d" % h, align_bytes=64)
+            scales = keep.tile([P, HALF], U8, name="scales%d" % h, align_bytes=64)
+            quarters = [slice(c, c + P) for c in range(0, HALF, P)]
+            for cols in quarters:
+                weave(h, 1, cols)
+            for cols in quarters:
+                nc.vector.quantize_mx(
+                    out=codes[:, cols].bitcast(FP8X4), scales=scales[:, cols],
+                    in_=grouped[h][:, cols, :].rearrange("p o t -> p (o t)"),
+                )
+            y = [psum.tile([P, HALF], F32, name="y%d%d" % (h, m), tag="y") for m in range(N // P)]
+            for cols in quarters:
+                for m in range(N // P):
+                    rows = slice(m * P, (m + 1) * P)
+                    nc.tensor.matmul_mx(
+                        out=y[m][:, cols], lhsT=vw[:, rows].bitcast(FP8X4), lhsT_scale=vsc[:, rows],
+                        rhs=codes[:, cols].bitcast(FP8X4), rhs_scale=scales[:, cols], start=True, stop=True,
+                    )
+            for m in range(N // P):
+                res = keep.tile([P, HALF], F32, name="res%d%d" % (h, m))
+                (nc.vector.tensor_copy if (h, m) == (1, 0) else nc.scalar.copy)(out=res[:], in_=y[m][:])
+                (nc.scalar if (h, m) == (1, 1) else nc.sync).dma_start(
+                    out=out[m * P : (m + 1) * P, h * HALF : (h + 1) * HALF], in_=res[:]
+                )
+
+        weave(0, 0, slice(0, HALF))
+        read_board(0, 1, "late")
+        read_board(1, 1, "late")
+        weave(1, 0, slice(0, HALF))
+        read_board(3, 0, "hid_first1")
+        read_board(2, 1, "x_words")
+        read_board(3, 1, "x_words")
+        finish(0)
+        finish(1)

@@ -47,11 +47,11 @@ def tile_picked_tokens_plain_twin_relaysum_store_plain_kernel(
 
         def load_plane(plane, scales):
             for q in range(QUADS):
-                nc.sync.dma_start(out=plane[32 * q : 32 * q + 4, :].bitcast(I32), in_=scales[0, 4 * q : 4 * q + 4, :].bitcast(I32))
+                (nc.scalar if q + 1 < QUADS else nc.sync).dma_start(out=plane[32 * q : 32 * q + 4, :].bitcast(I32), in_=scales[0, 4 * q : 4 * q + 4, :].bitcast(I32))
 
-        def stage_scales(scales, name):
+        def stage_scales(scales, name, tag):
             width = scales.shape[2]
-            staged = keep.tile([4, QUADS, width // 4], I32, name=name, tag="staged")
+            staged = keep.tile([4, QUADS, width // 4], I32, name=name, tag=tag, align_bytes=64)
             nc.sync.dma_start(out=staged[:], in_=scales[0].bitcast(I32).rearrange("(q r) c -> r q c", r=4))
             return staged
 
@@ -59,19 +59,21 @@ def tile_picked_tokens_plain_twin_relaysum_store_plain_kernel(
             for q in range(QUADS):
                 nc.vector.tensor_copy(out=plane[32 * q : 32 * q + 4, :].bitcast(I32), in_=staged[:, q, :])
 
-        def load_words(words, name):
+        def load_words(words, name, tag):
             width = words.shape[2]
-            raw = keep.tile([P, width], U32, name=name, tag="words", align_bytes=64)
+            raw = keep.tile([P, width], U32, name=name, tag=tag, align_bytes=64)
             nc.sync.dma_start(out=raw[:].bitcast(I32), in_=words[0].rearrange("p n t -> p (n t)").bitcast(I32))
             return raw
 
-        def load_rows(vec, name):
-            col = keep.tile([P, PACK], F32, name=name)
+        def load_rows(vec, name, tag):
+            col = keep.tile([P, PACK], F32, name=name, tag=tag, align_bytes=64)
             nc.sync.dma_start(out=col[:], in_=vec.rearrange("(p t) one -> p (t one)", t=PACK))
             return col
 
-        def deal(copy, raw, dealt, tiles):
-            copy(out=dealt[:, tiles, :], in_=raw[:].rearrange("p (m t) -> p t m", t=PACK)[:, tiles, :])
+        def deal(copy, raw, first, count, name, tag):
+            dealt = keep.tile([P, count, P], raw.dtype, name=name, tag=tag, align_bytes=64)
+            copy(out=dealt[:], in_=raw[:].rearrange("p (m t) -> p t m", t=PACK)[:, first : first + count, :])
+            return [dealt[:, i, :] for i in range(count)]
 
         def zero_board(width, name, tag):
             board = keep.tile([P, width], F32, name=name, tag=tag, align_bytes=64)
@@ -79,28 +81,25 @@ def tile_picked_tokens_plain_twin_relaysum_store_plain_kernel(
             return board
 
         xs_win = zero_plane(T, "xs_win", "x_scales")
-        load_plane(xs_win, xt_scales)
-        l_tok = load_list(offs, "l_tok")
-        ws_staged = stage_scales(w_scales, "ws_staged")
-        l_put_a = load_list(offs2, "l_put_a")
-        l_get_relay = load_list(offs3, "l_get_relay")
+        ws_staged = stage_scales(w_scales, "ws_staged", "w_staged")
         xw_win = keep.tile([P, T], U16, name="xw_win", tag="x_words", align_bytes=64)
         nc.sync.dma_start(out=xw_win[:].bitcast(I32), in_=xt_words[0].bitcast(I32))
-        ww_raw = load_words(w_words, "ww_raw")
-        sa_col = load_rows(sa, "sa_col")
+        load_plane(xs_win, xt_scales)
+        l_tok = load_list(offs, "l_tok")
+        ww_raw = load_words(w_words, "ww_raw", "w_words")
+        l_put_a = load_list(offs2, "l_put_a")
+        l_get_relay = load_list(offs3, "l_get_relay")
         l_put_b = load_list(offs5, "l_put_b")
         l_put_relay = load_list(offs4, "l_put_relay")
         l_get_hid = load_list(offs6, "l_get_hid")
-        sb_col = load_rows(sb, "sb_col")
         l_store = load_list(offs7, "l_store")
 
-        ws_raw = zero_plane(R, "ws_raw", "plane")
-        pw = zero_board(C, "pw", "pw")
+        ws_raw = zero_plane(R, "ws_raw", "w_plane")
+        pw = [zero_board(C, "pw0", "pw0")]
         spread_plane(ws_raw, ws_staged)
-        ws = keep.tile([P, PACK, P], U8, name="ws", align_bytes=64)
-        ww = keep.tile([P, PACK, P], U32, name="ww", align_bytes=64)
-        deal(nc.vector.tensor_copy, ws_raw, ws, slice(0, 1))
-        deal(nc.scalar.copy, ww_raw, ww, slice(0, PACK))
+        sa_col = load_rows(sa, "sa_col", "w_staged")
+        ws = deal(nc.vector.tensor_copy, ws_raw, 0, 1, "ws_first", "ws_dealt")
+        ww = deal(nc.scalar.copy, ww_raw, 0, 1, "ww_first", "ww_dealt")
 
         xw = keep.tile([P, J], U16, name="xw", align_bytes=64)
         xs = keep.tile([P, J], U8, name="xs", align_bytes=64)
@@ -109,7 +108,7 @@ def tile_picked_tokens_plain_twin_relaysum_store_plain_kernel(
             acc = psum.tile([P, count], F32, name="acc")
             cols = slice(first, first + count)
             nc.tensor.matmul_mx(
-                out=acc[:], lhsT=words[:, t, :].bitcast(FP8X4), lhsT_scale=scales[:, t, :],
+                out=acc[:], lhsT=words[t].bitcast(FP8X4), lhsT_scale=scales[t],
                 rhs=xw[:, cols].bitcast(FP4X4), rhs_scale=xs[:, cols], start=True, stop=True,
             )
             copy(out=dst[:, cols], in_=acc[:])
@@ -123,69 +122,70 @@ def tile_picked_tokens_plain_twin_relaysum_store_plain_kernel(
             nc.vector.tensor_copy(out=xw[:, cols], in_=xw_win[:].indirect(entries(l_tok, first, HALF)))
             nc.vector.tensor_copy(out=xs[:, cols], in_=xs_win[:].indirect(entries(l_tok, first, HALF)))
             product(ww, ws, 0, first, HALF, a[0], nc.scalar.copy if first == 0 else nc.vector.tensor_copy)
-        deal(nc.vector.tensor_copy, ws_raw, ws, slice(1, PACK))
-
-        w2w_raw = load_words(w2_words, "w2w_raw")
-        w2s_staged = stage_scales(w2_scales, "w2s_staged")
-        w2s_raw = zero_plane(R, "w2s_raw", "plane")
-        spread_plane(w2s_raw, w2s_staged)
-        w2s = keep.tile([P, PACK, P], U8, name="w2s", align_bytes=64)
-        w2w = keep.tile([P, PACK, P], U32, name="w2w", align_bytes=64)
-        deal(nc.vector.tensor_copy, w2s_raw, w2s, slice(0, PACK))
-        deal(nc.vector.tensor_copy, w2w_raw, w2w, slice(0, PACK))
-        pu = zero_board(D, "pu", "x_words")
-        pv = zero_board(D, "pv", "x_scales")
-        product(w2w, w2s, 0, 0, J, b[0], nc.vector.tensor_copy)
+        ws.extend(deal(nc.vector.tensor_copy, ws_raw, 1, PACK - 1, "ws_rest", "ws_dealt"))
+        ww.extend(deal(nc.vector.tensor_copy, ww_raw, 1, PACK - 1, "ww_rest", "ww_dealt"))
+        pw.append(zero_board(C, "pw1", "x_words"))
+        w2w_raw = load_words(w2_words, "w2w_raw", "w_words")
+        w2s_staged = stage_scales(w2_scales, "w2s_staged", "w_plane")
+        w2s_raw = zero_plane(R, "w2s_raw", "x_scales")
         for t in range(1, PACK):
             product(ww, ws, t, 0, J, a[t], nc.vector.tensor_copy)
-            product(w2w, w2s, t, 0, J, b[t], nc.vector.tensor_copy)
 
-        vsw_win = load_words(vs_words, "vsw_win")
-        vss_staged = stage_scales(vs_scales, "vss_staged")
-        vss_win = zero_plane(Z, "vss_win", "plane")
+        spread_plane(w2s_raw, w2s_staged)
+        w2s = deal(nc.vector.tensor_copy, w2s_raw, 0, PACK, "w2s", "w2s_dealt")
+        w2w = deal(nc.vector.tensor_copy, w2w_raw, 0, PACK, "w2w", "w2w_dealt")
+        pu = [zero_board(D, "pu0", "ww_dealt")]
+        pv = zero_board(D, "pv", "ws_dealt")
+        for t in range(PACK):
+            product(w2w, w2s, t, 0, J, b[t], nc.vector.tensor_copy)
+        pu.append(zero_board(D, "pu1", "x_scales"))
+
+        vsw_win = load_words(vs_words, "vsw_win", "w_words")
+        vss_staged = stage_scales(vs_scales, "vss_staged", "w_plane")
+        vss_win = zero_plane(Z, "vss_win", "w2s_dealt")
         spread_plane(vss_win, vss_staged)
+        sb_col = load_rows(sb, "sb_col", "w_plane")
         vw = keep.tile([P, N], U32, name="vw", align_bytes=64)
         vsc = keep.tile([P, N], U8, name="vsc", align_bytes=64)
         nc.vector.tensor_copy(out=vw[:], in_=vsw_win[:].indirect(l_store[:]))
         nc.vector.tensor_copy(out=vsc[:], in_=vss_win[:].indirect(l_store[:]))
 
-        h1 = keep.tile([P, S], F32, name="h1")
+        h1 = [keep.tile([P, S], F32, name="h1_%d" % i) for i in range(2)]
         pg = [keep.tile([P, D], F32, name="pg%d" % t) for t in range(PACK)]
-        hid = {}
 
-        def read_board(t, h, tag):
-            if t % 2 == 0:
-                hid[(h, t // 2)] = keep.tile([P, 2, HALF], BF16, name="hid%d%d" % (h, t // 2), tag=tag, align_bytes=64)
+        def put_a(t):
+            for first, count in ((0, HALF), (HALF, HALF)) if t == 0 else ((0, J),):
+                nc.scalar.activation(
+                    out=pw[t % 2][:].indirect(entries(l_put_a, first, count)), in_=a[t][:, first : first + count], func=COPY
+                )
+
+        def read_board(t, dst, first, count):
             nc.scalar.activation(
-                out=hid[(h, t // 2)][:, t % 2, :], in_=pg[t][:].indirect(entries(l_get_hid, h * HALF, HALF)),
-                func=COPY, scale=sb_col[:, t : t + 1],
+                out=dst, in_=pg[t][:].indirect(entries(l_get_hid, first, count)), func=COPY, scale=sb_col[:, t : t + 1]
             )
+
+        put_a(0)
+        for t in range(PACK):
+            if t + 1 < PACK:
+                put_a(t + 1)
+            nc.scalar.activation(
+                out=h1[t % 2][:], in_=pw[t % 2][:].indirect(l_get_relay[:]), func=COPY, scale=sa_col[:, t : t + 1]
+            )
+            nc.scalar.activation(out=pu[t % 2][:].indirect(l_put_b[:]), in_=b[t][:], func=COPY)
+            nc.scalar.activation(out=pv[:].indirect(l_put_relay[:]), in_=h1[t % 2][:], func=COPY)
+            nc.vector.tensor_tensor(out=pg[t][:], in0=pv[:], in1=pu[t % 2][:], op=ADD)
 
         grouped = [keep.tile([P, HALF, PACK], BF16, name="grouped%d" % h, align_bytes=64) for h in range(2)]
 
-        def weave(h, pair, cols):
-            nc.vector.tensor_copy(
-                out=grouped[h][:, cols, 2 * pair : 2 * pair + 2], in_=hid[(h, pair)][:, :, cols].rearrange("p t o -> p o t")
-            )
-
-        for t in range(PACK):
-            for first, count in ((0, HALF), (HALF, HALF)) if t == 0 else ((0, J),):
-                nc.scalar.activation(
-                    out=pw[:].indirect(entries(l_put_a, first, count)), in_=a[t][:, first : first + count], func=COPY
-                )
-            if t > 0:
-                read_board(t - 1, 0, "hid_first%d" % ((t - 1) // 2))
-            nc.scalar.activation(out=h1[:], in_=pw[:].indirect(l_get_relay[:]), func=COPY, scale=sa_col[:, t : t + 1])
-            nc.scalar.activation(out=pu[:].indirect(l_put_b[:]), in_=b[t][:], func=COPY)
-            nc.scalar.activation(out=pv[:].indirect(l_put_relay[:]), in_=h1[:], func=COPY)
-            nc.vector.tensor_tensor(out=pg[t][:], in0=pv[:], in1=pu[:], op=ADD)
+        def weave(h, pair, cols, src):
+            nc.vector.tensor_copy(out=grouped[h][:, cols, 2 * pair : 2 * pair + 2], in_=src.rearrange("p t o -> p o t"))
 
         def finish(h):
             codes = keep.tile([P, HALF], U32, name="codes%d" % h, align_bytes=64)
             scales = keep.tile([P, HALF], U8, name="scales%d" % h, align_bytes=64)
             quarters = [slice(c, c + P) for c in range(0, HALF, P)]
             for cols in quarters:
-                weave(h, 1, cols)
+                weave(h, 1, cols, hid_high[h][:, :, cols])
             for cols in quarters:
                 nc.vector.quantize_mx(
                     out=codes[:, cols].bitcast(FP8X4), scales=scales[:, cols],
@@ -206,12 +206,15 @@ def tile_picked_tokens_plain_twin_relaysum_store_plain_kernel(
                     out=out[m * P : (m + 1) * P, h * HALF : (h + 1) * HALF], in_=res[:]
                 )
 
-        weave(0, 0, slice(0, HALF))
-        read_board(0, 1, "late")
-        read_board(1, 1, "late")
-        weave(1, 0, slice(0, HALF))
-        read_board(3, 0, "hid_first1")
-        read_board(2, 1, "x_words")
-        read_board(3, 1, "x_words")
+        hid_low = keep.tile([P, 2, O], BF16, name="hid_low", tag="late", align_bytes=64)
+        for t in range(2):
+            read_board(t, hid_low[:, t, :], 0, O)
+        for h in range(2):
+            weave(h, 0, slice(0, HALF), hid_low[:, :, h * HALF : (h + 1) * HALF])
+        hid_high = []
+        for h, tag in enumerate(("hid_high", "x_scales")):
+            hid_high.append(keep.tile([P, 2, HALF], BF16, name="hid_high%d" % h, tag=tag, align_bytes=64))
+            for t in (2, 3):
+                read_board(t, hid_high[h][:, t - 2, :], h * HALF, HALF)
         finish(0)
         finish(1)

@@ -30,7 +30,7 @@ def tile_picked_tokens_plain_twin_relaysum_store_plain_kernel(
     nc = tc.nc
     with ExitStack() as ctx:
         keep = ctx.enter_context(tc.tile_pool(name="keep", bufs=1))
-        psum = ctx.enter_context(tc.psum_pool(name="psum", bufs=4))
+        psum = ctx.enter_context(tc.psum_pool(name="psum", bufs=8))
 
         def load_list(src, name):
             lst = keep.tile(list(src.shape), U16, name=name)
@@ -95,11 +95,12 @@ def tile_picked_tokens_plain_twin_relaysum_store_plain_kernel(
         l_store = load_list(offs7, "l_store")
 
         ws_raw = zero_plane(R, "ws_raw", "w_plane")
-        pw = [zero_board(C, "pw0", "pw0")]
+        pw = [zero_board(C, "pw%d" % i, "pw%d" % i) for i in range(2)]
         spread_plane(ws_raw, ws_staged)
         sa_col = load_rows(sa, "sa_col", "w_staged")
-        ws = deal(nc.vector.tensor_copy, ws_raw, 0, 1, "ws_first", "ws_dealt")
-        ww = deal(nc.scalar.copy, ww_raw, 0, 1, "ww_first", "ww_dealt")
+        ws = deal(nc.vector.tensor_copy, ws_raw, 0, 1, "ws_first", "ws_first")
+        ww = deal(nc.scalar.copy, ww_raw, 0, 1, "ww_first", "ww_first")
+        ww.extend(deal(nc.scalar.copy, ww_raw, 1, PACK - 1, "ww_rest", "ww_rest"))
 
         xw = keep.tile([P, J], U16, name="xw", align_bytes=64)
         xs = keep.tile([P, J], U8, name="xs", align_bytes=64)
@@ -122,9 +123,7 @@ def tile_picked_tokens_plain_twin_relaysum_store_plain_kernel(
             nc.vector.tensor_copy(out=xw[:, cols], in_=xw_win[:].indirect(entries(l_tok, first, HALF)))
             nc.vector.tensor_copy(out=xs[:, cols], in_=xs_win[:].indirect(entries(l_tok, first, HALF)))
             product(ww, ws, 0, first, HALF, a[0], nc.scalar.copy if first == 0 else nc.vector.tensor_copy)
-        ws.extend(deal(nc.vector.tensor_copy, ws_raw, 1, PACK - 1, "ws_rest", "ws_dealt"))
-        ww.extend(deal(nc.vector.tensor_copy, ww_raw, 1, PACK - 1, "ww_rest", "ww_dealt"))
-        pw.append(zero_board(C, "pw1", "x_words"))
+        ws.extend(deal(nc.vector.tensor_copy, ws_raw, 1, PACK - 1, "ws_rest", "x_words"))
         w2w_raw = load_words(w2_words, "w2w_raw", "w_words")
         w2s_staged = stage_scales(w2_scales, "w2s_staged", "w_plane")
         w2s_raw = zero_plane(R, "w2s_raw", "x_scales")
@@ -134,8 +133,8 @@ def tile_picked_tokens_plain_twin_relaysum_store_plain_kernel(
         spread_plane(w2s_raw, w2s_staged)
         w2s = deal(nc.vector.tensor_copy, w2s_raw, 0, PACK, "w2s", "w2s_dealt")
         w2w = deal(nc.vector.tensor_copy, w2w_raw, 0, PACK, "w2w", "w2w_dealt")
-        pu = [zero_board(D, "pu0", "ww_dealt")]
-        pv = zero_board(D, "pv", "ws_dealt")
+        pu = [zero_board(D, "pu0", "ww_rest")]
+        pv = zero_board(D, "pv", "x_words")
         for t in range(PACK):
             product(w2w, w2s, t, 0, J, b[t], nc.vector.tensor_copy)
         pu.append(zero_board(D, "pu1", "x_scales"))
@@ -177,44 +176,49 @@ def tile_picked_tokens_plain_twin_relaysum_store_plain_kernel(
 
         grouped = [keep.tile([P, HALF, PACK], BF16, name="grouped%d" % h, align_bytes=64) for h in range(2)]
 
-        def weave(h, pair, cols, src):
-            nc.vector.tensor_copy(out=grouped[h][:, cols, 2 * pair : 2 * pair + 2], in_=src.rearrange("p t o -> p o t"))
+        def weave(copy, h, pair, cols, src):
+            copy(out=grouped[h][:, cols, 2 * pair : 2 * pair + 2], in_=src.rearrange("p t o -> p o t"))
 
-        def finish(h):
+        quarters = [slice(c, c + P) for c in range(0, HALF, P)]
+
+        def quantise(h):
             codes = keep.tile([P, HALF], U32, name="codes%d" % h, align_bytes=64)
             scales = keep.tile([P, HALF], U8, name="scales%d" % h, align_bytes=64)
-            quarters = [slice(c, c + P) for c in range(0, HALF, P)]
-            for cols in quarters:
-                weave(h, 1, cols, hid_high[h][:, :, cols])
+            for i, cols in enumerate(quarters):
+                weave(nc.scalar.copy if (h, i) == (1, 1) else nc.vector.tensor_copy, h, 1, cols, hid_high[h][:, :, cols])
             for cols in quarters:
                 nc.vector.quantize_mx(
                     out=codes[:, cols].bitcast(FP8X4), scales=scales[:, cols],
                     in_=grouped[h][:, cols, :].rearrange("p o t -> p (o t)"),
                 )
-            y = [psum.tile([P, HALF], F32, name="y%d%d" % (h, m), tag="y") for m in range(N // P)]
+            return codes, scales
+
+        def emit(h, codes, scales):
+            res = [keep.tile([P, HALF], F32, name="res%d%d" % (h, m)) for m in range(N // P)]
             for cols in quarters:
                 for m in range(N // P):
                     rows = slice(m * P, (m + 1) * P)
+                    y = psum.tile([P, P], F32, name="y", tag="acc")
                     nc.tensor.matmul_mx(
-                        out=y[m][:, cols], lhsT=vw[:, rows].bitcast(FP8X4), lhsT_scale=vsc[:, rows],
+                        out=y[:], lhsT=vw[:, rows].bitcast(FP8X4), lhsT_scale=vsc[:, rows],
                         rhs=codes[:, cols].bitcast(FP8X4), rhs_scale=scales[:, cols], start=True, stop=True,
                     )
+                    (nc.vector.tensor_copy if (h, m) == (1, 0) else nc.scalar.copy)(out=res[m][:, cols], in_=y[:])
             for m in range(N // P):
-                res = keep.tile([P, HALF], F32, name="res%d%d" % (h, m))
-                (nc.vector.tensor_copy if (h, m) == (1, 0) else nc.scalar.copy)(out=res[:], in_=y[m][:])
                 (nc.scalar if (h, m) == (1, 1) else nc.sync).dma_start(
-                    out=out[m * P : (m + 1) * P, h * HALF : (h + 1) * HALF], in_=res[:]
+                    out=out[m * P : (m + 1) * P, h * HALF : (h + 1) * HALF], in_=res[m][:]
                 )
 
         hid_low = keep.tile([P, 2, O], BF16, name="hid_low", tag="late", align_bytes=64)
         for t in range(2):
             read_board(t, hid_low[:, t, :], 0, O)
         for h in range(2):
-            weave(h, 0, slice(0, HALF), hid_low[:, :, h * HALF : (h + 1) * HALF])
+            weave(nc.vector.tensor_copy, h, 0, slice(0, HALF), hid_low[:, :, h * HALF : (h + 1) * HALF])
         hid_high = []
         for h, tag in enumerate(("hid_high", "x_scales")):
             hid_high.append(keep.tile([P, 2, HALF], BF16, name="hid_high%d" % h, tag=tag, align_bytes=64))
             for t in (2, 3):
                 read_board(t, hid_high[h][:, t - 2, :], h * HALF, HALF)
-        finish(0)
-        finish(1)
+        quantised = [quantise(h) for h in range(2)]
+        for h in range(2):
+            emit(h, *quantised[h])

@@ -72,7 +72,7 @@ def tile_picked_tokens_plain_twin_relaysum_store_plain_kernel(
 
         def deal(copy, raw, first, count, name, tag):
             dealt = keep.tile([P, count, P], raw.dtype, name=name, tag=tag, align_bytes=64)
-            copy(out=dealt[:], in_=raw[:].rearrange("p (m t) -> p t m", t=PACK)[:, first : first + count, :])
+            copy(out=dealt[:], in_=raw[:, :].rearrange("p (m t) -> p t m", t=PACK)[:, first : first + count, :])
             return [dealt[:, i, :] for i in range(count)]
 
         def zero_board(width, name, tag):
@@ -94,11 +94,15 @@ def tile_picked_tokens_plain_twin_relaysum_store_plain_kernel(
         l_get_hid = load_list(offs6, "l_get_hid")
         l_store = load_list(offs7, "l_store")
 
-        ws_raw = zero_plane(R, "ws_raw", "w_plane")
+        ws_wide = zero_plane(2 * R, "ws_raw", "w_plane")
+        ws_raw = ws_wide[:, 0:R]
         pw = [zero_board(C, "pw%d" % i, "pw%d" % i) for i in range(2)]
-        spread_plane(ws_raw, ws_staged)
+        ws_view = ws_wide[:].bitcast(I32).rearrange("p (u c) -> p u c", u=2)
+        for q in range(2):
+            nc.vector.tensor_copy(out=ws_view[32 * q : 32 * q + 4, :, :], in_=ws_staged[:, q::2, :])
+        nc.vector.tensor_copy(out=ws_view[64:128, 0, :], in_=ws_view[0:64, 1, :])
         sa_col = load_rows(sa, "sa_col", "w_staged")
-        ws = deal(nc.vector.tensor_copy, ws_raw, 0, 1, "ws_first", "ws_first")
+        ws = deal(nc.gpsimd.tensor_copy, ws_raw, 0, 1, "ws_first", "ws_first")
         ww = deal(nc.scalar.copy, ww_raw, 0, 1, "ww_first", "ww_first")
         ww.extend(deal(nc.scalar.copy, ww_raw, 1, PACK - 1, "ww_rest", "ww_rest"))
 

from contextlib import ExitStack

import concourse.mybir as mybir

K, J, R, T, C, D, O, S, N, Z = 512, 512, 512, 2048, 1024, 1024, 512, 256, 256, 1024
FLOPS = 2 * (2 * K * R * J + R * N * O)

F32 = mybir.dt.float32
BF16 = mybir.dt.bfloat16
I32 = mybir.dt.int32
U32 = mybir.dt.uint32
U16 = mybir.dt.uint16
U8 = mybir.dt.uint8
FP8X4 = mybir.dt.float8_e4m3fn_x4
FP4X4 = mybir.dt.float4_e2m1fn_x4
COPY = mybir.ActivationFunctionType.Copy
ADD = mybir.AluOpType.add

P = 128
PACK = 4
QUADS = 4
STRIPE = 16
HALF = 256


def tile_picked_tokens_plain_twin_relaysum_store_plain_kernel(
    tc, xt_words, xt_scales, w_words, w_scales, w2_words, w2_scales, sa, sb, vs_words, vs_scales,
    offs, offs2, offs3, offs4, offs5, offs6, offs7, out,
):
    nc = tc.nc
    with ExitStack() as ctx:
        keep = ctx.enter_context(tc.tile_pool(name="keep", bufs=1))
        psum = ctx.enter_context(tc.psum_pool(name="psum", bufs=8))

        def load_list(src, name):
            lst = keep.tile(list(src.shape), U16, name=name)
            nc.sync.dma_start(lst[:], src)
            return lst

        def entries(lst, first, count):
            return lst[:, first // STRIPE : (first + count) // STRIPE]

        def zero_plane(width, name, tag):
            plane = keep.tile([P, width], U8, name=name, tag=tag, align_bytes=64)
            nc.vector.memset(plane[:].bitcast(I32), 0)
            return plane

        def load_plane(plane, scales):
            for q in range(QUADS):
                (nc.scalar if q + 1 < QUADS else nc.sync).dma_start(out=plane[32 * q : 32 * q + 4, :].bitcast(I32), in_=scales[0, 4 * q : 4 * q + 4, :].bitcast(I32))

        def stage_scales(scales, name, tag):
            width = scales.shape[2]
            staged = keep.tile([4, QUADS, width // 4], I32, name=name, tag=tag, align_bytes=64)
            nc.sync.dma_start(out=staged[:], in_=scales[0].bitcast(I32).rearrange("(q r) c -> r q c", r=4))
            return staged

        def spread_plane(plane, staged):
            for q in range(QUADS):
                nc.vector.tensor_copy(out=plane[32 * q : 32 * q + 4, :].bitcast(I32), in_=staged[:, q, :])

        def load_words(words, name, tag):
            width = words.shape[2]
            raw = keep.tile([P, width], U32, name=name, tag=tag, align_bytes=64)
            nc.sync.dma_start(out=raw[:].bitcast(I32), in_=words[0].rearrange("p n t -> p (n t)").bitcast(I32))
            return raw

        def load_rows(vec, name, tag):
            col = keep.tile([P, PACK], F32, name=name, tag=tag, align_bytes=64)
            nc.sync.dma_start(out=col[:], in_=vec.rearrange("(p t) one -> p (t one)", t=PACK))
            return col

        def deal(copy, raw, first, count, name, tag):
            dealt = keep.tile([P, count, P], raw.dtype, name=name, tag=tag, align_bytes=64)
            copy(out=dealt[:], in_=raw[:, :].rearrange("p (m t) -> p t m", t=PACK)[:, first : first + count, :])
            return [dealt[:, i, :] for i in range(count)]

        def zero_board(width, name, tag):
            board = keep.tile([P, width], F32, name=name, tag=tag, align_bytes=64)
            nc.vector.memset(board[:], 0.0)
            return board

        xs_win = zero_plane(T, "xs_win", "x_scales")
        ws_staged = stage_scales(w_scales, "ws_staged", "w_staged")
        xw_win = keep.tile([P, T], U16, name="xw_win", tag="x_words", align_bytes=64)
        nc.sync.dma_start(out=xw_win[:].bitcast(I32), in_=xt_words[0].bitcast(I32))
        load_plane(xs_win, xt_scales)
        l_tok = load_list(offs, "l_tok")
        ww_raw = load_words(w_words, "ww_raw", "w_words")
        l_put_a = load_list(offs2, "l_put_a")
        l_get_relay = load_list(offs3, "l_get_relay")
        l_put_b = load_list(offs5, "l_put_b")
        l_put_relay = load_list(offs4, "l_put_relay")
        l_get_hid = load_list(offs6, "l_get_hid")
        l_store = load_list(offs7, "l_store")

        ws_wide = zero_plane(2 * R, "ws_raw", "w_plane")
        ws_raw = ws_wide[:, 0:R]
        pw = [zero_board(C, "pw%d" % i, "pw%d" % i) for i in range(2)]
        ws_view = ws_wide[:].bitcast(I32).rearrange("p (u c) -> p u c", u=2)
        for q in range(2):
            nc.vector.tensor_copy(out=ws_view[32 * q : 32 * q + 4, :, :], in_=ws_staged[:, q::2, :])
        nc.vector.tensor_copy(out=ws_view[64:128, 0, :], in_=ws_view[0:64, 1, :])
        sa_col = load_rows(sa, "sa_col", "w_staged")
        ws = deal(nc.gpsimd.tensor_copy, ws_raw, 0, 1, "ws_first", "ws_first")
        ww = deal(nc.scalar.copy, ww_raw, 0, 1, "ww_first", "ww_first")
        ww.extend(deal(nc.scalar.copy, ww_raw, 1, PACK - 1, "ww_rest", "ww_rest"))

        xw = keep.tile([P, J], U16, name="xw", align_bytes=64)
        xs = keep.tile([P, J], U8, name="xs", align_bytes=64)

        def product(words, scales, t, first, count, dst, copy):
            acc = psum.tile([P, count], F32, name="acc")
            cols = slice(first, first + count)
            nc.tensor.matmul_mx(
                out=acc[:], lhsT=words[t].bitcast(FP8X4), lhsT_scale=scales[t],
                rhs=xw[:, cols].bitcast(FP4X4), rhs_scale=xs[:, cols], start=True, stop=True,
            )
            copy(out=dst[:, cols], in_=acc[:])

        a = [keep.tile([P, J], F32, name="a%d" % t) for t in range(PACK)]
        b = [keep.tile([P, J], F32, name="b%d" % t) for t in range(PACK - 1)]
        b.append(keep.tile([P, J], F32, name="b_last", tag="late", align_bytes=64))

        for first in (0, HALF):
            cols = slice(first, first + HALF)
            nc.vector.tensor_copy(out=xw[:, cols], in_=xw_win[:].indirect(entries(l_tok, first, HALF)))
            nc.vector.tensor_copy(out=xs[:, cols], in_=xs_win[:].indirect(entries(l_tok, first, HALF)))
            product(ww, ws, 0, first, HALF, a[0], nc.scalar.copy if first == 0 else nc.vector.tensor_copy)
        ws.extend(deal(nc.vector.tensor_copy, ws_raw, 1, PACK - 1, "ws_rest", "x_words"))
        w2w_raw = load_words(w2_words, "w2w_raw", "w_words")
        w2s_staged = stage_scales(w2_scales, "w2s_staged", "w_plane")
        w2s_raw = zero_plane(R, "w2s_raw", "x_scales")
        for t in range(1, PACK):
            product(ww, ws, t, 0, J, a[t], nc.vector.tensor_copy)

        spread_plane(w2s_raw, w2s_staged)
        w2s = deal(nc.vector.tensor_copy, w2s_raw, 0, PACK, "w2s", "w2s_dealt")
        w2w = deal(nc.vector.tensor_copy, w2w_raw, 0, PACK, "w2w", "w2w_dealt")
        pu = [zero_board(D, "pu0", "ww_rest")]
        pv = zero_board(D, "pv", "x_words")
        for t in range(PACK):
            product(w2w, w2s, t, 0, J, b[t], nc.vector.tensor_copy)
        pu.append(zero_board(D, "pu1", "x_scales"))

        vsw_win = load_words(vs_words, "vsw_win", "w_words")
        vss_staged = stage_scales(vs_scales, "vss_staged", "w_plane")
        vss_win = zero_plane(Z, "vss_win", "w2s_dealt")
        spread_plane(vss_win, vss_staged)
        sb_col = load_rows(sb, "sb_col", "w_plane")
        vw = keep.tile([P, N], U32, name="vw", align_bytes=64)
        vsc = keep.tile([P, N], U8, name="vsc", align_bytes=64)
        nc.vector.tensor_copy(out=vw[:], in_=vsw_win[:].indirect(l_store[:]))
        nc.vector.tensor_copy(out=vsc[:], in_=vss_win[:].indirect(l_store[:]))

        h1 = [keep.tile([P, S], F32, name="h1_%d" % i) for i in range(2)]
        pg = [keep.tile([P, D], F32, name="pg%d" % t) for t in range(PACK)]

        def put_a(t):
            for first, count in ((0, HALF), (HALF, HALF)) if t == 0 else ((0, J),):
                nc.scalar.activation(
                    out=pw[t % 2][:].indirect(entries(l_put_a, first, count)), in_=a[t][:, first : first + count], func=COPY
                )

        def read_board(t, dst, first, count):
            nc.scalar.activation(
                out=dst, in_=pg[t][:].indirect(entries(l_get_hid, first, count)), func=COPY, scale=sb_col[:, t : t + 1]
            )

        put_a(0)
        for t in range(PACK):
            if t + 1 < PACK:
                put_a(t + 1)
            nc.scalar.activation(
                out=h1[t % 2][:], in_=pw[t % 2][:].indirect(l_get_relay[:]), func=COPY, scale=sa_col[:, t : t + 1]
            )
            nc.scalar.activation(out=pu[t % 2][:].indirect(l_put_b[:]), in_=b[t][:], func=COPY)
            nc.scalar.activation(out=pv[:].indirect(l_put_relay[:]), in_=h1[t % 2][:], func=COPY)
            nc.vector.tensor_tensor(out=pg[t][:], in0=pv[:], in1=pu[t % 2][:], op=ADD)

        grouped = [keep.tile([P, HALF, PACK], BF16, name="grouped%d" % h, align_bytes=64) for h in range(2)]

        def weave(copy, h, pair, cols, src):
            copy(out=grouped[h][:, cols, 2 * pair : 2 * pair + 2], in_=src.rearrange("p t o -> p o t"))

        quarters = [slice(c, c + P) for c in range(0, HALF, P)]

        def quantise(h):
            codes = keep.tile([P, HALF], U32, name="codes%d" % h, align_bytes=64)
            scales = keep.tile([P, HALF], U8, name="scales%d" % h, align_bytes=64)
            for i, cols in enumerate(quarters):
                weave(nc.scalar.copy if (h, i) == (1, 1) else nc.vector.tensor_copy, h, 1, cols, hid_high[h][:, :, cols])
            for cols in quarters:
                nc.vector.quantize_mx(
                    out=codes[:, cols].bitcast(FP8X4), scales=scales[:, cols],
                    in_=grouped[h][:, cols, :].rearrange("p o t -> p (o t)"),
                )
            return codes, scales

        def emit(h, codes, scales):
            res = [keep.tile([P, HALF], F32, name="res%d%d" % (h, m)) for m in range(N // P)]
            for cols in quarters:
                for m in range(N // P):
                    rows = slice(m * P, (m + 1) * P)
                    y = psum.tile([P, P], F32, name="y", tag="acc")
                    nc.tensor.matmul_mx(
                        out=y[:], lhsT=vw[:, rows].bitcast(FP8X4), lhsT_scale=vsc[:, rows],
                        rhs=codes[:, cols].bitcast(FP8X4), rhs_scale=scales[:, cols], start=True, stop=True,
                    )
                    (nc.vector.tensor_copy if (h, m) == (1, 0) else nc.scalar.copy)(out=res[m][:, cols], in_=y[:])
            for m in range(N // P):
                (nc.scalar if (h, m) == (1, 1) else nc.sync).dma_start(
                    out=out[m * P : (m + 1) * P, h * HALF : (h + 1) * HALF], in_=res[m][:]
                )

        hid_low = keep.tile([P, 2, O], BF16, name="hid_low", tag="late", align_bytes=64)
        for t in range(2):
            read_board(t, hid_low[:, t, :], 0, O)
        for h in range(2):
            weave(nc.vector.tensor_copy, h, 0, slice(0, HALF), hid_low[:, :, h * HALF : (h + 1) * HALF])
        hid_high = []
        for h, tag in enumerate(("hid_high", "x_scales")):
            hid_high.append(keep.tile([P, 2, HALF], BF16, name="hid_high%d" % h, tag=tag, align_bytes=64))
            for t in (2, 3):
                read_board(t, hid_high[h][:, t - 2, :], h * HALF, HALF)
        quantised = [quantise(h) for h in range(2)]
        for h in range(2):
            emit(h, *quantised[h])
